import numpy as np
import ml_dtypes


def mxq(x, axis, fmt="e4m3"):
    dtype, down = {"e4m3": (ml_dtypes.float8_e4m3fn, 7), "e5m2": (ml_dtypes.float8_e5m2, 14)}[fmt]
    v = np.moveaxis(np.asarray(x, np.float32).astype(ml_dtypes.bfloat16).astype(np.float64), axis, -1)
    blocks = v.reshape(v.shape[:-1] + (-1, 32))
    amax = np.abs(blocks).max(-1, keepdims=True)
    byte = np.maximum(np.where(amax > 0, np.frexp(amax)[1] - 1 + 127, 0) - down, 1)
    scale = np.exp2(byte - 127.0)
    codes = (blocks / scale).astype(np.float32).astype(dtype).astype(np.float64)
    return np.moveaxis((codes * scale).reshape(v.shape), -1, axis)


WIDE = False


def mx_kscale(k):
    if not WIDE:
        return np.ones(k)
    levels = np.array([10, -10, 5, -5, 0])
    if k % 512:
        return np.exp2(np.random.permutation(np.resize(levels, k // 32))).repeat(32)
    a = np.empty((k // 512, 16))
    for p in range(k // 512):
        a[p, :8] = np.random.permutation(np.resize(levels, 8))
        for g in range(8):
            far = levels[np.abs(levels - a[p, g]) >= 10]
            a[p, g + 8] = far[np.random.randint(len(far))]
    return np.exp2(a.ravel()).repeat(32)


def f64(x):
    return np.asarray(x).astype(np.float64)


def striped8(idx):
    return np.concatenate([v.reshape(-1, 16).T for v in idx]).astype(np.uint16)


def unstriped8(offs):
    return np.stack([offs[16 * g:16 * g + 16].T.reshape(-1) for g in range(8)]).astype(np.int64)


E2M1 = np.array([0.0, 0.5, 1.0, 1.5, 2.0, 3.0, 4.0, 6.0, -0.0, -0.5, -1.0, -1.5, -2.0, -3.0, -4.0, -6.0])


def pack_weight(w, fmt):
    k, n = w.shape
    w = f64(np.asarray(w, np.float32).astype(ml_dtypes.bfloat16)).reshape(k // 32, 32, n)
    amax = np.abs(w).max(1)
    if fmt == "e4m3":
        byte = np.frexp(amax)[1] - 1 + 127 - 7
    else:
        mant, ex = np.frexp(amax / 6.0)
        byte = np.where(mant > 0.5, ex, ex - 1) + 127
    byte = np.clip(np.where(amax > 0, byte, 1), 1, 254)
    scaled = (w * np.exp2(127.0 - byte)[:, None, :]).reshape(k, n).astype(np.float32)
    by_word = np.ascontiguousarray(scaled.reshape(k // 512, 128, 4, n).transpose(0, 1, 3, 2))
    if fmt == "e4m3":
        words = by_word.astype(ml_dtypes.float8_e4m3fn).view(np.uint8)
    else:
        c = by_word.astype(ml_dtypes.float4_e2m1fn).view(np.uint8) & 0xF
        words = (c[..., 0::2] | (c[..., 1::2] << 4)).reshape(k // 512, 128, 2 * n)
    return np.ascontiguousarray(words), np.ascontiguousarray(byte.astype(np.uint8).reshape(k // 512, 16, n))


def unpack_weight(words, scales, fmt):
    g, _, n = scales.shape
    words = np.ascontiguousarray(words).reshape(g, 128, n, -1)
    if fmt == "e4m3":
        vals = words.view(ml_dtypes.float8_e4m3fn).astype(np.float64)
    else:
        nib = np.empty((g, 128, n, 4), np.uint8)
        nib[..., 0::2] = words & 0xF
        nib[..., 1::2] = words >> 4
        vals = E2M1[nib]
    vals = vals * np.repeat(np.exp2(scales.astype(np.float64) - 127.0), 8, axis=1)[..., None]
    return vals.transpose(0, 1, 3, 2).reshape(g * 512, n)


K, M, T, S = 512, 1024, 512, 256


def setup_inputs():
    n = np.random.standard_normal
    s = mx_kscale(K)[:, None]
    p_w = pack_weight(n((K, M)) / np.sqrt(K) / s, "e4m3")
    return {
        "x": (n((K, S)) * s).astype(np.float32),
        "w_words": p_w[0],
        "w_scales": p_w[1],
        "b": (0.3 * n(1024)).astype(np.float32),
        "wgo": np.repeat(np.random.uniform(0.5, 2.0, (8, S)), 16, axis=0).astype(np.float32),
        "offs": striped8(np.stack([np.random.permutation(T)[:S] for _ in range(8)])),
    }


def reference(x, w_words, w_scales, b, wgo, offs):
    x_ = mxq(f64(x), 0, "e4m3")
    w_ = unpack_weight(w_words, w_scales, "e4m3")
    y = w_.T @ x_
    place = unstriped8(offs)[np.arange(M) % 128 // 16]
    out = np.zeros((M, T))
    out[np.arange(M)[:, None], place] = f64(wgo)[np.arange(M) % 128] * (y + f64(b)[:, None])
    return out

@@ -1,0 +1,134 @@
+from contextlib import ExitStack
+
+import concourse.mybir as mybir
+from concourse.masks import make_identity
+
+K, M, T, S = 512, 1024, 512, 256
+FLOPS = 2 * K * M * S
+
+P = 128
+BLOCKS = M // P
+HALF = 128
+F32 = mybir.dt.float32
+BF16 = mybir.dt.bfloat16
+I32 = mybir.dt.int32
+U32 = mybir.dt.uint32
+U16 = mybir.dt.uint16
+U8 = mybir.dt.uint8
+FP8X4 = mybir.dt.float8_e4m3fn_x4
+MULT = mybir.AluOpType.mult
+IDENTITY = mybir.ActivationFunctionType.Identity
+
+
+def tile_list_hscat_bias_kernel(tc, x, w_words, w_scales, b, wgo, offs, out):
+    nc = tc.nc
+    with ExitStack() as ctx:
+        keep = ctx.enter_context(tc.tile_pool(name="keep", bufs=1))
+        wpool = ctx.enter_context(tc.tile_pool(name="wpool", bufs=6))
+        ypool = ctx.enter_context(tc.tile_pool(name="ypool", bufs=6))
+        psum = ctx.enter_context(tc.psum_pool(name="psum", bufs=6))
+        bpsum = ctx.enter_context(tc.psum_pool(name="bpsum", bufs=1))
+
+        offsets = keep.tile([P, S // 16], U16, name="offsets")
+
+        xv = x.rearrange("(p j) w -> p j w", j=4)
+        raw = [keep.tile([P, 4, HALF], F32, name=f"raw{h}") for h in range(2)]
+        w_bytes = w_words[0].rearrange("p n t -> p (n t)")
+        w_first = keep.tile([P, P], U32, name="w_first", align_bytes=64)
+        w_rest = keep.tile([P, M - P], U32, name="w_rest", align_bytes=64)
+        w_sc = keep.tile([P, M], U8, name="w_sc", align_bytes=64)
+        wgo_sb = keep.tile([P, S], F32, name="wgo_sb")
+        b_rows = keep.tile([P, P], F32, name="b_rows")
+        bias = keep.tile([P, BLOCKS], F32, name="bias")
+        ident = keep.tile([P, P], F32, name="ident")
+        warm = keep.tile([P, 1], F32, name="warm")
+
+        nc.gpsimd.memset(b_rows[:], 0.0)
+        nc.vector.memset(w_sc[:].bitcast(I32), 0)
+        nc.vector.memset(warm[:], 0.0)
+        nc.sync.dma_start(raw[0][:], xv[:, :, 0:HALF])
+        nc.scalar.dma_start(w_first[:].bitcast(I32), w_bytes[:, 0 : 4 * P].bitcast(I32))
+        for q in range(4):
+            nc.scalar.dma_start(
+                w_sc[32 * q : 32 * q + 4, :].bitcast(I32), w_scales[0][4 * q : 4 * q + 4, :].bitcast(I32)
+            )
+        nc.sync.dma_start(offsets[:], offs)
+        nc.sync.dma_start(wgo_sb[:], wgo)
+        nc.gpsimd.dma_start(b_rows[0:BLOCKS, :], b.rearrange("(c p) -> c p", p=P))
+        nc.gpsimd.dma_start(w_rest[:].bitcast(I32), w_bytes[:, 4 * P : 4 * M].bitcast(I32))
+        nc.sync.dma_start(raw[1][:], xv[:, :, HALF:S])
+        make_identity(nc, ident[:])
+        nc.scalar.activation(warm[:], warm[:], IDENTITY, bias=warm[:])
+
+        windows = {}
+
+        def clear(c, engine):
+            windows[c] = wpool.tile([P, T], F32, name="window")
+            engine.memset(windows[c][:], 0.0)
+
+        for c in range(4):
+            clear(c, nc.vector)
+        for c in (4, 5):
+            clear(c, nc.gpsimd)
+
+        b_turned = bpsum.tile([P, P], F32, name="b_turned")
+        nc.tensor.transpose(b_turned[:], b_rows[:], ident[:])
+        nc.scalar.copy(bias[:], b_turned[:, 0:BLOCKS])
+
+        codes = [keep.tile([P, HALF], U32, name=f"codes{h}", align_bytes=64) for h in range(2)]
+        scales = [keep.tile([P, HALF], U8, name=f"scales{h}", align_bytes=64) for h in range(2)]
+        grouped = [keep.tile([P, HALF, 4], BF16, name=f"grouped{h}", align_bytes=64) for h in range(2)]
+
+        def cast(h, engine_copy):
+            engine_copy(
+                grouped[h][:].rearrange("p (c i) t -> p c t i", i=4),
+                raw[h][:].rearrange("p t (c i) -> p c t i", i=4),
+            )
+
+        def quantize(h):
+            nc.vector.quantize_mx(
+                out=codes[h][:].bitcast(FP8X4),
+                scales=scales[h][:],
+                in_=grouped[h][:].rearrange("p w t -> p (w t)"),
+            )
+
+        def product(c, h):
+            acc = psum.tile([P, HALF], F32, name="acc")
+            lhs = w_first[:] if c == 0 else w_rest[:, P * (c - 1) : P * c]
+            nc.tensor.matmul_mx(
+                out=acc[:],
+                lhsT=lhs.bitcast(FP8X4),
+                lhsT_scale=w_sc[:, P * c : P * (c + 1)],
+                rhs=codes[h][:].bitcast(FP8X4),
+                rhs_scale=scales[h][:],
+                start=True,
+                stop=True,
+            )
+            y = ypool.tile([P, HALF], F32, name="y")
+            nc.scalar.activation(y[:], acc[:], IDENTITY, bias=bias[:, c : c + 1])
+            return y
+
+        def place(c, h):
+            y = product(c, h)
+            nc.vector.tensor_tensor(
+                windows[c][:].indirect(offsets[:, 8 * h : 8 * h + 8]), y[:], wgo_sb[:, HALF * h : HALF * (h + 1)], MULT
+            )
+            if h == 1:
+                nc.sync.dma_start(out[P * c : P * (c + 1), :], windows[c][:])
+
+        cast(0, nc.vector.tensor_copy)
+        quantize(0)
+        cast(1, nc.scalar.copy)
+        place(0, 0)
+        place(1, 0)
+        place(2, 0)
+        quantize(1)
+        place(3, 0)
+        for c in range(4):
+            place(c, 1)
+        for c in (6, 7):
+            clear(c, nc.gpsimd)
+        for pair in (4, 6):
+            for h in range(2):
+                for c in (pair, pair + 1):
+                    place(c, h)

@@ -32,10 +32,9 @@ def tile_list_hscat_bias_kernel(tc, x, w_words, w_scales, b, wgo, offs, out):
         offsets = keep.tile([P, S // 16], U16, name="offsets")
 
         xv = x.rearrange("(p j) w -> p j w", j=4)
-        raw = [keep.tile([P, 4, HALF], F32, name=f"raw{h}") for h in range(2)]
+        raw = keep.tile([P, 4, S], F32, name="raw")
         w_bytes = w_words[0].rearrange("p n t -> p (n t)")
-        w_first = keep.tile([P, P], U32, name="w_first", align_bytes=64)
-        w_rest = keep.tile([P, M - P], U32, name="w_rest", align_bytes=64)
+        w_codes = keep.tile([P, M], U32, name="w_codes", align_bytes=64)
         w_sc = keep.tile([P, M], U8, name="w_sc", align_bytes=64)
         wgo_sb = keep.tile([P, S], F32, name="wgo_sb")
         b_rows = keep.tile([P, P], F32, name="b_rows")
@@ -44,19 +43,16 @@ def tile_list_hscat_bias_kernel(tc, x, w_words, w_scales, b, wgo, offs, out):
         warm = keep.tile([P, 1], F32, name="warm")
 
         nc.gpsimd.memset(b_rows[:], 0.0)
-        nc.vector.memset(w_sc[:].bitcast(I32), 0)
-        nc.vector.memset(warm[:], 0.0)
-        nc.sync.dma_start(raw[0][:], xv[:, :, 0:HALF])
-        nc.scalar.dma_start(w_first[:].bitcast(I32), w_bytes[:, 0 : 4 * P].bitcast(I32))
+        nc.gpsimd.memset(warm[:], 0.0)
+        nc.sync.dma_start(offsets[:], offs)
+        nc.sync.dma_start(raw[:], xv)
+        nc.sync.dma_start(b_rows[0:BLOCKS, :], b.rearrange("(c p) -> c p", p=P))
         for q in range(4):
             nc.scalar.dma_start(
                 w_sc[32 * q : 32 * q + 4, :].bitcast(I32), w_scales[0][4 * q : 4 * q + 4, :].bitcast(I32)
             )
-        nc.sync.dma_start(offsets[:], offs)
-        nc.sync.dma_start(wgo_sb[:], wgo)
-        nc.gpsimd.dma_start(b_rows[0:BLOCKS, :], b.rearrange("(c p) -> c p", p=P))
-        nc.gpsimd.dma_start(w_rest[:].bitcast(I32), w_bytes[:, 4 * P : 4 * M].bitcast(I32))
-        nc.sync.dma_start(raw[1][:], xv[:, :, HALF:S])
+        nc.scalar.dma_start(w_codes[:].bitcast(I32), w_bytes.bitcast(I32))
+        nc.gpsimd.dma_start(wgo_sb[:], wgo)
         make_identity(nc, ident[:])
         nc.scalar.activation(warm[:], warm[:], IDENTITY, bias=warm[:])
 
@@ -82,7 +78,7 @@ def tile_list_hscat_bias_kernel(tc, x, w_words, w_scales, b, wgo, offs, out):
         def cast(h, engine_copy):
             engine_copy(
                 grouped[h][:].rearrange("p (c i) t -> p c t i", i=4),
-                raw[h][:].rearrange("p t (c i) -> p c t i", i=4),
+                raw[:, :, HALF * h : HALF * (h + 1)].rearrange("p t (c i) -> p c t i", i=4),
             )
 
         def quantize(h):
@@ -94,10 +90,9 @@ def tile_list_hscat_bias_kernel(tc, x, w_words, w_scales, b, wgo, offs, out):
 
         def product(c, h):
             acc = psum.tile([P, HALF], F32, name="acc")
-            lhs = w_first[:] if c == 0 else w_rest[:, P * (c - 1) : P * c]
             nc.tensor.matmul_mx(
                 out=acc[:],
-                lhsT=lhs.bitcast(FP8X4),
+                lhsT=w_codes[:, P * c : P * (c + 1)].bitcast(FP8X4),
                 lhsT_scale=w_sc[:, P * c : P * (c + 1)],
                 rhs=codes[h][:].bitcast(FP8X4),
                 rhs_scale=scales[h][:],
@@ -117,18 +112,13 @@ def tile_list_hscat_bias_kernel(tc, x, w_words, w_scales, b, wgo, offs, out):
                 nc.sync.dma_start(out[P * c : P * (c + 1), :], windows[c][:])
 
         cast(0, nc.vector.tensor_copy)
-        quantize(0)
         cast(1, nc.scalar.copy)
-        place(0, 0)
-        place(1, 0)
-        place(2, 0)
+        quantize(0)
         quantize(1)
-        place(3, 0)
-        for c in range(4):
-            place(c, 1)
-        for c in (6, 7):
-            clear(c, nc.gpsimd)
-        for pair in (4, 6):
+        for pair in range(0, BLOCKS, 2):
+            if pair == 6:
+                clear(6, nc.gpsimd)
+                clear(7, nc.gpsimd)
             for h in range(2):
                 for c in (pair, pair + 1):
                     place(c, h)

from contextlib import ExitStack

import concourse.mybir as mybir
from concourse.masks import make_identity

K, M, T, S = 512, 1024, 512, 256
FLOPS = 2 * K * M * S

P = 128
BLOCKS = M // P
HALF = 128
F32 = mybir.dt.float32
BF16 = mybir.dt.bfloat16
I32 = mybir.dt.int32
U32 = mybir.dt.uint32
U16 = mybir.dt.uint16
U8 = mybir.dt.uint8
FP8X4 = mybir.dt.float8_e4m3fn_x4
MULT = mybir.AluOpType.mult
IDENTITY = mybir.ActivationFunctionType.Identity


def tile_list_hscat_bias_kernel(tc, x, w_words, w_scales, b, wgo, offs, out):
    nc = tc.nc
    with ExitStack() as ctx:
        keep = ctx.enter_context(tc.tile_pool(name="keep", bufs=1))
        wpool = ctx.enter_context(tc.tile_pool(name="wpool", bufs=6))
        ypool = ctx.enter_context(tc.tile_pool(name="ypool", bufs=6))
        psum = ctx.enter_context(tc.psum_pool(name="psum", bufs=6))
        bpsum = ctx.enter_context(tc.psum_pool(name="bpsum", bufs=1))

        offsets = keep.tile([P, S // 16], U16, name="offsets")

        xv = x.rearrange("(p j) w -> p j w", j=4)
        raw = keep.tile([P, 4, S], F32, name="raw")
        w_bytes = w_words[0].rearrange("p n t -> p (n t)")
        w_codes = keep.tile([P, M], U32, name="w_codes", align_bytes=64)
        w_sc = keep.tile([P, M], U8, name="w_sc", align_bytes=64)
        wgo_sb = keep.tile([P, S], F32, name="wgo_sb")
        b_rows = keep.tile([P, P], F32, name="b_rows")
        bias = keep.tile([P, BLOCKS], F32, name="bias")
        ident = keep.tile([P, P], F32, name="ident")
        warm = keep.tile([P, 1], F32, name="warm")

        nc.gpsimd.memset(b_rows[:], 0.0)
        nc.gpsimd.memset(warm[:], 0.0)
        nc.sync.dma_start(offsets[:], offs)
        nc.sync.dma_start(raw[:], xv)
        nc.sync.dma_start(b_rows[0:BLOCKS, :], b.rearrange("(c p) -> c p", p=P))
        for q in range(4):
            nc.scalar.dma_start(
                w_sc[32 * q : 32 * q + 4, :].bitcast(I32), w_scales[0][4 * q : 4 * q + 4, :].bitcast(I32)
            )
        nc.scalar.dma_start(w_codes[:].bitcast(I32), w_bytes.bitcast(I32))
        nc.gpsimd.dma_start(wgo_sb[:], wgo)
        make_identity(nc, ident[:])
        nc.scalar.activation(warm[:], warm[:], IDENTITY, bias=warm[:])

        windows = {}

        def clear(c, engine):
            windows[c] = wpool.tile([P, T], F32, name="window")
            engine.memset(windows[c][:], 0.0)

        for c in range(4):
            clear(c, nc.vector)
        for c in (4, 5):
            clear(c, nc.gpsimd)

        b_turned = bpsum.tile([P, P], F32, name="b_turned")
        nc.tensor.transpose(b_turned[:], b_rows[:], ident[:])
        nc.scalar.copy(bias[:], b_turned[:, 0:BLOCKS])

        codes = [keep.tile([P, HALF], U32, name=f"codes{h}", align_bytes=64) for h in range(2)]
        scales = [keep.tile([P, HALF], U8, name=f"scales{h}", align_bytes=64) for h in range(2)]
        grouped = [keep.tile([P, HALF, 4], BF16, name=f"grouped{h}", align_bytes=64) for h in range(2)]

        def cast(h, engine_copy):
            engine_copy(
                grouped[h][:].rearrange("p (c i) t -> p c t i", i=4),
                raw[:, :, HALF * h : HALF * (h + 1)].rearrange("p t (c i) -> p c t i", i=4),
            )

        def quantize(h):
            nc.vector.quantize_mx(
                out=codes[h][:].bitcast(FP8X4),
                scales=scales[h][:],
                in_=grouped[h][:].rearrange("p w t -> p (w t)"),
            )

        def product(c, h):
            acc = psum.tile([P, HALF], F32, name="acc")
            nc.tensor.matmul_mx(
                out=acc[:],
                lhsT=w_codes[:, P * c : P * (c + 1)].bitcast(FP8X4),
                lhsT_scale=w_sc[:, P * c : P * (c + 1)],
                rhs=codes[h][:].bitcast(FP8X4),
                rhs_scale=scales[h][:],
                start=True,
                stop=True,
            )
            y = ypool.tile([P, HALF], F32, name="y")
            nc.scalar.activation(y[:], acc[:], IDENTITY, bias=bias[:, c : c + 1])
            return y

        def place(c, h):
            y = product(c, h)
            nc.vector.tensor_tensor(
                windows[c][:].indirect(offsets[:, 8 * h : 8 * h + 8]), y[:], wgo_sb[:, HALF * h : HALF * (h + 1)], MULT
            )
            if h == 1:
                nc.sync.dma_start(out[P * c : P * (c + 1), :], windows[c][:])

        cast(0, nc.vector.tensor_copy)
        cast(1, nc.scalar.copy)
        quantize(0)
        quantize(1)
        for pair in range(0, BLOCKS, 2):
            if pair == 6:
                clear(6, nc.gpsimd)
                clear(7, nc.gpsimd)
            for h in range(2):
                for c in (pair, pair + 1):
                    place(c, h)
